import numpy as np
import ml_dtypes


def mxq(x, axis, fmt="e4m3"):
    dtype, down = {"e4m3": (ml_dtypes.float8_e4m3fn, 7), "e5m2": (ml_dtypes.float8_e5m2, 14)}[fmt]
    v = np.moveaxis(np.asarray(x, np.float32).astype(ml_dtypes.bfloat16).astype(np.float64), axis, -1)
    blocks = v.reshape(v.shape[:-1] + (-1, 32))
    amax = np.abs(blocks).max(-1, keepdims=True)
    byte = np.maximum(np.where(amax > 0, np.frexp(amax)[1] - 1 + 127, 0) - down, 1)
    scale = np.exp2(byte - 127.0)
    codes = (blocks / scale).astype(np.float32).astype(dtype).astype(np.float64)
    return np.moveaxis((codes * scale).reshape(v.shape), -1, axis)


WIDE = False


def mx_kscale(k):
    if not WIDE:
        return np.ones(k)
    levels = np.array([10, -10, 5, -5, 0])
    if k % 512:
        return np.exp2(np.random.permutation(np.resize(levels, k // 32))).repeat(32)
    a = np.empty((k // 512, 16))
    for p in range(k // 512):
        a[p, :8] = np.random.permutation(np.resize(levels, 8))
        for g in range(8):
            far = levels[np.abs(levels - a[p, g]) >= 10]
            a[p, g + 8] = far[np.random.randint(len(far))]
    return np.exp2(a.ravel()).repeat(32)


def f64(x):
    return np.asarray(x).astype(np.float64)


def striped(idx):
    return np.tile(idx.reshape(-1, 16).T, (8, 1)).astype(np.uint16)


def unstriped(offs):
    return offs[:16].T.reshape(-1).astype(np.int64)


def pack_weight(w):
    k, n = w.shape
    w = f64(np.asarray(w, np.float32).astype(ml_dtypes.bfloat16)).reshape(k // 32, 32, n)
    amax = np.abs(w).max(1)
    byte = np.clip(np.where(amax > 0, np.frexp(amax)[1] - 1 + 127 - 7, 1), 1, 254)
    scaled = (w * np.exp2(127.0 - byte)[:, None, :]).reshape(k, n).astype(np.float32)
    words = np.ascontiguousarray(scaled.reshape(k // 512, 128, 4, n).transpose(0, 1, 3, 2)).astype(ml_dtypes.float8_e4m3fn).view(np.uint8)
    return words, np.ascontiguousarray(byte.astype(np.uint8).reshape(k // 512, 16, n))


def unpack_weight(words, scales):
    g, p, n, _ = words.shape
    vals = np.ascontiguousarray(words).view(ml_dtypes.float8_e4m3fn).astype(np.float64) * np.repeat(np.exp2(scales.astype(np.float64) - 127.0), 8, axis=1)[..., None]
    return vals.transpose(0, 1, 3, 2).reshape(g * 512, n)


def relu(v):
    return np.maximum(v, 0.0)


K, T, S, D, H, N, V, U = 512, 1024, 512, 4, 512, 128, 128, 512
P = 2 ** 7


def setup_inputs():
    n = np.random.standard_normal
    s = mx_kscale(K)[:, None]
    u = mx_kscale(H)
    packed_xT = pack_weight(n((K, T)) * s)
    return {
        "x_words": packed_xT[0],
        "x_scales": packed_xT[1],
        "w1": (n((K, H)) / np.sqrt(K) / s * u).astype(np.float32),
        "w2": (n((H, N)) / np.sqrt(H) / u[:, None]).astype(np.float32),
        "accel": (n((N, S))).astype(np.float32),
        "dt": (np.tile(np.random.uniform(0.2, 0.6, S), (P, 1))).astype(np.float32),
        "lev": (np.tile(np.random.uniform(0.1, 1.0, S), (P, 1))).astype(np.float32),
        "vel": (n((N, U))).astype(np.float32),
        "posi": (n((N, U))).astype(np.float32),
        "tt": (np.tile(np.random.uniform(0.8, 2.0, V), (P, 1))).astype(np.float32),
        "offs": striped(np.random.permutation(T)[:S]),
        "from1": striped(np.random.randint(0, U, V)),
        "to1": striped(np.random.randint(0, U, V)),
    }


def reference(x_words, x_scales, w1, w2, accel, dt, lev, vel, posi, tt, offs, from1, to1):
    xq = unpack_weight(x_words, x_scales)[:, unstriped(offs)]
    h = relu(mxq(f64(w1), 0, "e4m3").T @ xq)
    a0 = f64(accel) + 0.3 * ((mxq(f64(w2), 0, "e4m3").T @ mxq(h, 0, "e4m3")))
    ap = a0 * f64(lev)[:1]
    dp = ap.reshape(len(ap), -1, D).sum(axis=2)
    rp = f64(posi)[:, unstriped(to1)] - f64(posi)[:, unstriped(from1)] - (f64(vel)[:, unstriped(from1)] * f64(tt)[:1]) - dp
    av = a0 * f64(dt)[:1]
    dv = av.reshape(len(av), -1, D).sum(axis=2)
    rv = f64(vel)[:, unstriped(to1)] - f64(vel)[:, unstriped(from1)] - dv
    return rp + 0.5 * rv

@@ -1,0 +1,177 @@
+import concourse.mybir as mybir
+from concourse.masks import make_identity
+
+F32 = mybir.dt.float32
+BF16 = mybir.dt.bfloat16
+I32 = mybir.dt.int32
+U32 = mybir.dt.uint32
+U16 = mybir.dt.uint16
+U8 = mybir.dt.uint8
+FP8X4 = mybir.dt.float8_e4m3fn_x4
+ALU = mybir.AluOpType
+ACT = mybir.ActivationFunctionType
+AXIS = mybir.AxisListType
+
+P = 128
+PACK = 4
+T, S, H, V, U, D = 1024, 512, 512, 128, 512, 4
+CHUNK = 128
+NCHUNK = S // CHUNK
+VC = CHUNK // D
+QUARTER = H // 4
+MQ = QUARTER // PACK
+
+FLOPS = 2 * 512 * H * S + 2 * H * P * S
+
+
+def tile_picked_yimu_res_p_kernel(
+    tc, x_words, x_scales, w1, w2, accel, dt, lev, vel, posi, tt, offs, from1, to1, out
+):
+    nc = tc.nc
+    with tc.tile_pool(name="sb", bufs=1) as sb, tc.psum_pool(name="ps", bufs=1) as ps:
+        offs_t = sb.tile([P, S // 16], U16, name="offs_t")
+        from_t = sb.tile([P, V // 16], U16, name="from_t")
+        to_t = sb.tile([P, V // 16], U16, name="to_t")
+        xw = sb.tile([P, T], U32, name="xw", align_bytes=64)
+        xs = sb.tile([P, T], U8, name="xs", align_bytes=64)
+
+        nc.vector.memset(xs[:].bitcast(I32), 0)
+        nc.sync.dma_start(offs_t[:], offs)
+        nc.sync.dma_start(xw[:].bitcast(I32), x_words[0].rearrange("p n t -> p (n t)").bitcast(I32))
+        for q in range(4):
+            nc.sync.dma_start(
+                xs[32 * q : 32 * q + 4, :].bitcast(I32), x_scales[0, 4 * q : 4 * q + 4, :].bitcast(I32)
+            )
+        w1v = w1.rearrange("(p j) c -> p j c", j=PACK)
+        w1raw = []
+        for q in range(4):
+            raw = sb.tile([P, PACK, QUARTER], F32, name="w1raw%d" % q)
+            nc.sync.dma_start(raw[:], w1v[:, :, q * QUARTER : (q + 1) * QUARTER])
+            w1raw.append(raw)
+        w2raw = sb.tile([P, PACK, P], F32, name="w2raw")
+        nc.sync.dma_start(w2raw[:], w2.rearrange("(p j) m -> p j m", j=PACK))
+        tt_t = sb.tile([P, V], F32, name="tt_t")
+        nc.sync.dma_start(tt_t[:], tt)
+        nc.sync.dma_start(from_t[:], from1)
+        nc.sync.dma_start(to_t[:], to1)
+        vel_t = sb.tile([P, U], F32, name="vel_t")
+        posi_t = sb.tile([P, U], F32, name="posi_t")
+        acc_t = sb.tile([P, S], F32, name="acc_t")
+        nc.sync.dma_start(vel_t[:], vel)
+        nc.sync.dma_start(posi_t[:], posi)
+        nc.sync.dma_start(acc_t[:], accel)
+
+        lev_s = sb.tile([P, D], F32, name="lev_s")
+        dt_s = sb.tile([P, D], F32, name="dt_s")
+        nc.gpsimd.dma_start(lev_s[:], lev[0:1, :].rearrange("o (v d) -> (o v) d", d=D))
+        nc.gpsimd.dma_start(dt_s[:], dt[0:1, :].rearrange("o (v d) -> (o v) d", d=D))
+
+        ident = sb.tile([P, P], F32, name="ident")
+        make_identity(nc, ident[:])
+        half_dt = sb.tile([P, D], F32, name="half_dt")
+        coef_s = sb.tile([P, D], F32, name="coef_s")
+        nc.gpsimd.tensor_scalar(half_dt[:], dt_s[:], 0.5, 0.0, ALU.mult, ALU.add)
+        nc.gpsimd.tensor_tensor(coef_s[:], half_dt[:], lev_s[:], ALU.add)
+        coef = ps.tile([P, D, V], F32, name="coef")
+        for d in range(D):
+            nc.tensor.transpose(coef[:, d, :], coef_s[:, d : d + 1].to_broadcast([P, P]), ident[:])
+        tt2 = sb.tile([P, V], F32, name="tt2")
+        nc.gpsimd.tensor_scalar(tt2[:], tt_t[:], 2.0, 1.0, ALU.mult, ALU.add)
+
+        gs = sb.tile([P, S], U8, name="gs", align_bytes=64)
+        gw = sb.tile([P, S], U32, name="gw", align_bytes=64)
+        nc.vector.tensor_copy(gs[:], xs[:].indirect(offs_t[:]))
+        nc.vector.tensor_copy(gw[:], xw[:].indirect(offs_t[:]))
+
+        w1c = sb.tile([P, PACK, P], U32, name="w1c", align_bytes=64)
+        w1s = sb.tile([P, PACK, P], U8, name="w1s", align_bytes=64)
+        for half in range(2):
+            grp = sb.tile([P, PACK, 2 * MQ, PACK], BF16, name="w1g%d" % half, align_bytes=64)
+            for i in range(2):
+                q = 2 * half + i
+                dst = grp[:, :, i * MQ : (i + 1) * MQ, :].rearrange("p t m j -> p m t j")
+                src = w1raw[q][:].rearrange("p j (m t) -> p m t j", t=PACK)
+                if q == 3:
+                    nc.vector.tensor_copy(dst, src)
+                else:
+                    nc.scalar.activation(dst, src, ACT.Copy)
+            cols = slice(half * 2 * MQ, (half + 1) * 2 * MQ)
+            for t in range(PACK):
+                nc.vector.quantize_mx(
+                    out=w1c[:, t, cols].bitcast(FP8X4),
+                    scales=w1s[:, t, cols],
+                    in_=grp[:, t, :, :].rearrange("p m j -> p (m j)"),
+                )
+
+        w2g = sb.tile([P, P, PACK], BF16, name="w2g", align_bytes=64)
+        nc.scalar.activation(
+            w2g[:].rearrange("p (c i) j -> p c j i", i=4),
+            w2raw[:].rearrange("p j (c i) -> p c j i", i=4),
+            ACT.Copy,
+        )
+        w2c = sb.tile([P, P], U32, name="w2c", align_bytes=64)
+        w2s = sb.tile([P, P], U8, name="w2s", align_bytes=64)
+        nc.vector.quantize_mx(out=w2c[:].bitcast(FP8X4), scales=w2s[:], in_=w2g[:].rearrange("p m j -> p (m j)"))
+
+        za = sb.tile([P, V], F32, name="za")
+        zb = sb.tile([P, V], F32, name="zb")
+        zx = sb.tile([P, V], F32, name="zx")
+        zy = sb.tile([P, V], F32, name="zy")
+        zz = sb.tile([P, V], F32, name="zz")
+        nc.vector.tensor_tensor(za[:], vel_t[:].indirect(from_t[:]), tt2[:], ALU.mult)
+        nc.vector.tensor_tensor(zb[:], vel_t[:].indirect(to_t[:]), za[:], ALU.subtract)
+        nc.gpsimd.tensor_scalar(zx[:], zb[:], 0.5, 0.0, ALU.mult, ALU.add)
+        nc.vector.tensor_tensor(zy[:], posi_t[:].indirect(from_t[:]), zx[:], ALU.subtract)
+        nc.vector.tensor_tensor(zz[:], posi_t[:].indirect(to_t[:]), zy[:], ALU.subtract)
+
+        hq = []
+        for c in range(NCHUNK):
+            cols = slice(c * CHUNK, (c + 1) * CHUNK)
+            hp = ps.tile([P, PACK, CHUNK], F32, name="hp%d" % c, tag="bank%d" % c)
+            for t in range(PACK):
+                nc.tensor.matmul_mx(
+                    out=hp[:, t, :],
+                    lhsT=w1c[:, t, :].bitcast(FP8X4),
+                    lhsT_scale=w1s[:, t, :],
+                    rhs=gw[:, cols].bitcast(FP8X4),
+                    rhs_scale=gs[:, cols],
+                    start=True,
+                    stop=True,
+                )
+            hg = sb.tile([P, CHUNK, PACK], BF16, name="hg%d" % c, align_bytes=64)
+            nc.scalar.activation(hg[:], hp[:].rearrange("p t n -> p n t"), ACT.Relu)
+            hc = sb.tile([P, CHUNK], U32, name="hc%d" % c, align_bytes=64)
+            hs = sb.tile([P, CHUNK], U8, name="hs%d" % c, align_bytes=64)
+            nc.vector.quantize_mx(out=hc[:].bitcast(FP8X4), scales=hs[:], in_=hg[:].rearrange("p n t -> p (n t)"))
+            hq.append((hc, hs))
+
+        dsum = sb.tile([P, V], F32, name="dsum")
+        res = sb.tile([P, V], F32, name="res")
+        for c in range(NCHUNK):
+            cols = slice(c * CHUNK, (c + 1) * CHUNK)
+            vcols = slice(c * VC, (c + 1) * VC)
+            hc, hs = hq[c]
+            yp = ps.tile([P, CHUNK], F32, name="yp%d" % c, tag="bank%d" % c)
+            nc.tensor.matmul_mx(
+                out=yp[:],
+                lhsT=w2c[:].bitcast(FP8X4),
+                lhsT_scale=w2s[:],
+                rhs=hc[:].bitcast(FP8X4),
+                rhs_scale=hs[:],
+                start=True,
+                stop=True,
+            )
+            a0 = sb.tile([P, CHUNK], F32, name="a0_%d" % c)
+            nc.vector.scalar_tensor_tensor(a0[:], yp[:], 0.3, acc_t[:, cols], ALU.mult, ALU.add)
+            wa = sb.tile([P, VC, D], F32, name="wa%d" % c)
+            nc.vector.tensor_tensor(
+                wa[:],
+                a0[:].rearrange("p (v d) -> p v d", d=D),
+                coef[:, :, vcols].rearrange("p d v -> p v d"),
+                ALU.mult,
+            )
+            nc.vector.tensor_reduce(dsum[:, vcols], wa[:], AXIS.X, ALU.add)
+        last = (NCHUNK - 1) * VC
+        nc.vector.tensor_tensor(res[:, :last], zz[:, :last], dsum[:, :last], ALU.subtract)
+        nc.vector.tensor_tensor(res[:, last:], zz[:, last:], dsum[:, last:], ALU.subtract)
+        nc.sync.dma_start(out, res[:])

@@ -18,8 +18,8 @@ T, S, H, V, U, D = 1024, 512, 512, 128, 512, 4
 CHUNK = 128
 NCHUNK = S // CHUNK
 VC = CHUNK // D
-QUARTER = H // 4
-MQ = QUARTER // PACK
+HALF = H // 2
+MH = HALF // PACK
 
 FLOPS = 2 * 512 * H * S + 2 * H * P * S
 
@@ -36,74 +36,67 @@ def tile_picked_yimu_res_p_kernel(
         xs = sb.tile([P, T], U8, name="xs", align_bytes=64)
 
         nc.vector.memset(xs[:].bitcast(I32), 0)
+        xs_in = sb.tile([P, T], U8, name="xs_in", align_bytes=64)
+        for q in range(4):
+            rows = slice(32 * q, 32 * q + 4)
+            queue = nc.sync if q < 2 else nc.scalar
+            queue.dma_start(xs_in[rows, :].bitcast(I32), x_scales[0, 4 * q : 4 * q + 4, :].bitcast(I32))
+            nc.vector.tensor_copy(xs[rows, :].bitcast(I32), xs_in[rows, :].bitcast(I32))
         nc.sync.dma_start(offs_t[:], offs)
         nc.sync.dma_start(xw[:].bitcast(I32), x_words[0].rearrange("p n t -> p (n t)").bitcast(I32))
-        for q in range(4):
-            nc.sync.dma_start(
-                xs[32 * q : 32 * q + 4, :].bitcast(I32), x_scales[0, 4 * q : 4 * q + 4, :].bitcast(I32)
-            )
         w1v = w1.rearrange("(p j) c -> p j c", j=PACK)
-        w1raw = []
-        for q in range(4):
-            raw = sb.tile([P, PACK, QUARTER], F32, name="w1raw%d" % q)
-            nc.sync.dma_start(raw[:], w1v[:, :, q * QUARTER : (q + 1) * QUARTER])
-            w1raw.append(raw)
-        w2raw = sb.tile([P, PACK, P], F32, name="w2raw")
-        nc.sync.dma_start(w2raw[:], w2.rearrange("(p j) m -> p j m", j=PACK))
+        w1a = sb.tile([P, PACK, HALF], F32, name="w1a")
+        w1b = sb.tile([P, PACK, HALF], F32, name="w1b", tag="slot5", align_bytes=64)
+        lev_s = sb.tile([P, D], F32, name="lev_s")
+        dt_s = sb.tile([P, D], F32, name="dt_s")
+        w2raw = sb.tile([P, PACK, P], F32, name="w2raw", tag="slot6", align_bytes=64)
         tt_t = sb.tile([P, V], F32, name="tt_t")
-        nc.sync.dma_start(tt_t[:], tt)
-        nc.sync.dma_start(from_t[:], from1)
-        nc.sync.dma_start(to_t[:], to1)
         vel_t = sb.tile([P, U], F32, name="vel_t")
         posi_t = sb.tile([P, U], F32, name="posi_t")
         acc_t = sb.tile([P, S], F32, name="acc_t")
-        nc.sync.dma_start(vel_t[:], vel)
+        nc.sync.dma_start(w1a[:], w1v[:, :, :HALF])
+        nc.sync.dma_start(lev_s[:], lev[0:1, :].rearrange("o (v d) -> (o v) d", d=D))
+        nc.sync.dma_start(dt_s[:], dt[0:1, :].rearrange("o (v d) -> (o v) d", d=D))
+        nc.sync.dma_start(w1b[:], w1v[:, :, HALF:])
+        nc.sync.dma_start(w2raw[:], w2.rearrange("(p j) m -> p j m", j=PACK))
+        nc.sync.dma_start(from_t[:], from1)
+        nc.sync.dma_start(to_t[:], to1)
         nc.sync.dma_start(posi_t[:], posi)
+        nc.sync.dma_start(tt_t[:], tt)
+        nc.sync.dma_start(vel_t[:], vel)
         nc.sync.dma_start(acc_t[:], accel)
-
-        lev_s = sb.tile([P, D], F32, name="lev_s")
-        dt_s = sb.tile([P, D], F32, name="dt_s")
-        nc.gpsimd.dma_start(lev_s[:], lev[0:1, :].rearrange("o (v d) -> (o v) d", d=D))
-        nc.gpsimd.dma_start(dt_s[:], dt[0:1, :].rearrange("o (v d) -> (o v) d", d=D))
 
         ident = sb.tile([P, P], F32, name="ident")
         make_identity(nc, ident[:])
-        half_dt = sb.tile([P, D], F32, name="half_dt")
-        coef_s = sb.tile([P, D], F32, name="coef_s")
-        nc.gpsimd.tensor_scalar(half_dt[:], dt_s[:], 0.5, 0.0, ALU.mult, ALU.add)
-        nc.gpsimd.tensor_tensor(coef_s[:], half_dt[:], lev_s[:], ALU.add)
-        coef = ps.tile([P, D, V], F32, name="coef")
-        for d in range(D):
-            nc.tensor.transpose(coef[:, d, :], coef_s[:, d : d + 1].to_broadcast([P, P]), ident[:])
-        tt2 = sb.tile([P, V], F32, name="tt2")
-        nc.gpsimd.tensor_scalar(tt2[:], tt_t[:], 2.0, 1.0, ALU.mult, ALU.add)
 
         gs = sb.tile([P, S], U8, name="gs", align_bytes=64)
         gw = sb.tile([P, S], U32, name="gw", align_bytes=64)
         nc.vector.tensor_copy(gs[:], xs[:].indirect(offs_t[:]))
         nc.vector.tensor_copy(gw[:], xw[:].indirect(offs_t[:]))
 
-        w1c = sb.tile([P, PACK, P], U32, name="w1c", align_bytes=64)
-        w1s = sb.tile([P, PACK, P], U8, name="w1s", align_bytes=64)
+        w1c = [sb.tile([P, P], U32, name="w1c%d" % t, align_bytes=64) for t in range(PACK)]
+        w1s = [sb.tile([P, P], U8, name="w1s%d" % t, align_bytes=64) for t in range(PACK)]
+        ga = sb.tile([P, PACK - 1, MH, PACK], BF16, name="ga", align_bytes=64)
+        gd = sb.tile([P, MH, PACK], BF16, name="gd", align_bytes=64)
+        gb = sb.tile([P, PACK - 1, MH, PACK], BF16, name="gb", tag="slot0", align_bytes=64)
+        gc = sb.tile([P, MH, PACK], BF16, name="gc", tag="slot1", align_bytes=64)
+        src_a = w1a[:].rearrange("p j (m t) -> p m t j", t=PACK)
+        src_b = w1b[:].rearrange("p j (m t) -> p m t j", t=PACK)
+        nc.scalar.activation(ga[:].rearrange("p t m j -> p m t j"), src_a[:, :, : PACK - 1, :], ACT.Copy)
+        nc.vector.tensor_copy(gd[:], src_a[:, :, PACK - 1, :])
+        nc.vector.tensor_copy(gb[:].rearrange("p t m j -> p m t j"), src_b[:, :, : PACK - 1, :])
+        nc.scalar.activation(gc[:], src_b[:, :, PACK - 1, :], ACT.Copy)
         for half in range(2):
-            grp = sb.tile([P, PACK, 2 * MQ, PACK], BF16, name="w1g%d" % half, align_bytes=64)
-            for i in range(2):
-                q = 2 * half + i
-                dst = grp[:, :, i * MQ : (i + 1) * MQ, :].rearrange("p t m j -> p m t j")
-                src = w1raw[q][:].rearrange("p j (m t) -> p m t j", t=PACK)
-                if q == 3:
-                    nc.vector.tensor_copy(dst, src)
-                else:
-                    nc.scalar.activation(dst, src, ACT.Copy)
-            cols = slice(half * 2 * MQ, (half + 1) * 2 * MQ)
             for t in range(PACK):
+                cols = slice(half * MH, (half + 1) * MH)
+                grouped = (ga, gb)[half][:, t] if t < PACK - 1 else (gd, gc)[half][:]
                 nc.vector.quantize_mx(
-                    out=w1c[:, t, cols].bitcast(FP8X4),
-                    scales=w1s[:, t, cols],
-                    in_=grp[:, t, :, :].rearrange("p m j -> p (m j)"),
+                    out=w1c[t][:, cols].bitcast(FP8X4),
+                    scales=w1s[t][:, cols],
+                    in_=grouped.rearrange("p m j -> p (m j)"),
                 )
 
-        w2g = sb.tile([P, P, PACK], BF16, name="w2g", align_bytes=64)
+        w2g = sb.tile([P, P, PACK], BF16, name="w2g", tag="slot5", align_bytes=64)
         nc.scalar.activation(
             w2g[:].rearrange("p (c i) j -> p c j i", i=4),
             w2raw[:].rearrange("p j (c i) -> p c j i", i=4),
@@ -113,47 +106,53 @@ def tile_picked_yimu_res_p_kernel(
         w2s = sb.tile([P, P], U8, name="w2s", align_bytes=64)
         nc.vector.quantize_mx(out=w2c[:].bitcast(FP8X4), scales=w2s[:], in_=w2g[:].rearrange("p m j -> p (m j)"))
 
-        za = sb.tile([P, V], F32, name="za")
-        zb = sb.tile([P, V], F32, name="zb")
-        zx = sb.tile([P, V], F32, name="zx")
-        zy = sb.tile([P, V], F32, name="zy")
-        zz = sb.tile([P, V], F32, name="zz")
-        nc.vector.tensor_tensor(za[:], vel_t[:].indirect(from_t[:]), tt2[:], ALU.mult)
-        nc.vector.tensor_tensor(zb[:], vel_t[:].indirect(to_t[:]), za[:], ALU.subtract)
-        nc.gpsimd.tensor_scalar(zx[:], zb[:], 0.5, 0.0, ALU.mult, ALU.add)
-        nc.vector.tensor_tensor(zy[:], posi_t[:].indirect(from_t[:]), zx[:], ALU.subtract)
-        nc.vector.tensor_tensor(zz[:], posi_t[:].indirect(to_t[:]), zy[:], ALU.subtract)
+        coef_s = sb.tile([P, D], F32, name="coef_s")
+        half_dt = sb.tile([P, D], F32, name="half_dt")
+        nc.gpsimd.tensor_scalar(half_dt[:], dt_s[:], 0.5, 0.0, ALU.mult, ALU.add)
+        nc.gpsimd.tensor_tensor(coef_s[:], half_dt[:], lev_s[:], ALU.add)
+        coef = ps.tile([P, D, V], F32, name="coef")
+        for d in range(D):
+            nc.tensor.transpose(coef[:, d, :], coef_s[:, d : d + 1].to_broadcast([P, P]), ident[:])
+        tt2 = sb.tile([P, V], F32, name="tt2")
+        nc.gpsimd.tensor_scalar(tt2[:], tt_t[:], 2.0, 1.0, ALU.mult, ALU.add)
+        last = (NCHUNK - 1) * VC
+        lastj = (NCHUNK - 1) * CHUNK
+        coef_last = coef[:, :, last:].rearrange("p d v -> p v d")
+        ycoef = sb.tile([P, VC, D], F32, name="ycoef", tag="slot6", align_bytes=64)
+        nc.scalar.activation(ycoef[:], coef_last, ACT.Copy, scale=-0.3)
 
-        hq = []
+        hg = []
         for c in range(NCHUNK):
             cols = slice(c * CHUNK, (c + 1) * CHUNK)
             hp = ps.tile([P, PACK, CHUNK], F32, name="hp%d" % c, tag="bank%d" % c)
             for t in range(PACK):
                 nc.tensor.matmul_mx(
                     out=hp[:, t, :],
-                    lhsT=w1c[:, t, :].bitcast(FP8X4),
-                    lhsT_scale=w1s[:, t, :],
+                    lhsT=w1c[t][:].bitcast(FP8X4),
+                    lhsT_scale=w1s[t][:],
                     rhs=gw[:, cols].bitcast(FP8X4),
                     rhs_scale=gs[:, cols],
                     start=True,
                     stop=True,
                 )
-            hg = sb.tile([P, CHUNK, PACK], BF16, name="hg%d" % c, align_bytes=64)
-            nc.scalar.activation(hg[:], hp[:].rearrange("p t n -> p n t"), ACT.Relu)
-            hc = sb.tile([P, CHUNK], U32, name="hc%d" % c, align_bytes=64)
-            hs = sb.tile([P, CHUNK], U8, name="hs%d" % c, align_bytes=64)
-            nc.vector.quantize_mx(out=hc[:].bitcast(FP8X4), scales=hs[:], in_=hg[:].rearrange("p n t -> p (n t)"))
-            hq.append((hc, hs))
+            g = sb.tile([P, CHUNK, PACK], BF16, name="hg%d" % c, tag="hg%d" % c, align_bytes=64)
+            nc.scalar.activation(g[:], hp[:].rearrange("p t n -> p n t"), ACT.Relu)
+            hg.append(g)
 
-        dsum = sb.tile([P, V], F32, name="dsum")
-        res = sb.tile([P, V], F32, name="res")
-        for c in range(NCHUNK):
-            cols = slice(c * CHUNK, (c + 1) * CHUNK)
-            vcols = slice(c * VC, (c + 1) * VC)
-            hc, hs = hq[c]
-            yp = ps.tile([P, CHUNK], F32, name="yp%d" % c, tag="bank%d" % c)
+        za = sb.tile([P, V], F32, name="za", tag="slot1", align_bytes=64)
+        zx = sb.tile([P, V], F32, name="zx", tag="slot0", align_bytes=64)
+        zb = sb.tile([P, V], F32, name="zb")
+        zy = sb.tile([P, V], F32, name="zy")
+        zz = sb.tile([P, V], F32, name="zz")
+        nc.vector.tensor_copy(zx[:], posi_t[:].indirect(from_t[:]))
+        nc.vector.tensor_tensor(zy[:], posi_t[:].indirect(to_t[:]), zx[:], ALU.subtract)
+
+        def second_layer(c, yp, codes_tag):
+            hc = sb.tile([P, CHUNK], U32, name="hc%d" % c, tag=codes_tag, align_bytes=64)
+            hs = sb.tile([P, CHUNK], U8, name="hs%d" % c, align_bytes=64)
+            nc.vector.quantize_mx(out=hc[:].bitcast(FP8X4), scales=hs[:], in_=hg[c][:].rearrange("p n t -> p (n t)"))
             nc.tensor.matmul_mx(
-                out=yp[:],
+                out=yp,
                 lhsT=w2c[:].bitcast(FP8X4),
                 lhsT_scale=w2s[:],
                 rhs=hc[:].bitcast(FP8X4),
@@ -161,17 +160,49 @@ def tile_picked_yimu_res_p_kernel(
                 start=True,
                 stop=True,
             )
-            a0 = sb.tile([P, CHUNK], F32, name="a0_%d" % c)
-            nc.vector.scalar_tensor_tensor(a0[:], yp[:], 0.3, acc_t[:, cols], ALU.mult, ALU.add)
-            wa = sb.tile([P, VC, D], F32, name="wa%d" % c)
+
+        dsum = sb.tile([P, V], F32, name="dsum")
+        res = sb.tile([P, V], F32, name="res")
+        terms = sb.tile([P, VC, 2 * D], F32, name="terms")
+
+        def correct(v0, v1, yp):
+            a0 = sb.tile([P, (v1 - v0) * D], F32, name="a0_%d" % v0, tag="a0")
+            nc.vector.scalar_tensor_tensor(a0[:], yp, 0.3, acc_t[:, v0 * D : v1 * D], ALU.mult, ALU.add)
+            return a0
+
+        def weigh(v0, v1, values, tag):
+            wa = sb.tile([P, v1 - v0, D], F32, name="wa%d" % v0, tag=tag, align_bytes=64)
             nc.vector.tensor_tensor(
                 wa[:],
-                a0[:].rearrange("p (v d) -> p v d", d=D),
-                coef[:, :, vcols].rearrange("p d v -> p v d"),
+                values.rearrange("p (v d) -> p v d", d=D),
+                coef[:, :, v0:v1].rearrange("p d v -> p v d"),
                 ALU.mult,
             )
-            nc.vector.tensor_reduce(dsum[:, vcols], wa[:], AXIS.X, ALU.add)
-        last = (NCHUNK - 1) * VC
+            return wa
+
+        def total(v0, v1, wa):
+            nc.vector.tensor_reduce(dsum[:, v0:v1], wa[:], AXIS.X, ALU.add)
+
+        y01 = ps.tile([P, 2 * CHUNK], F32, name="y01", tag="bank0")
+        y2 = ps.tile([P, CHUNK], F32, name="y2", tag="bank1")
+        y3 = ps.tile([P, CHUNK], F32, name="y3", tag="bank2")
+        nc.vector.tensor_tensor(za[:], vel_t[:].indirect(from_t[:]), tt2[:], ALU.mult)
+        second_layer(0, y01[:, :CHUNK], "slot0")
+        nc.vector.tensor_tensor(zb[:], vel_t[:].indirect(to_t[:]), za[:], ALU.subtract)
+        second_layer(1, y01[:, CHUNK:], "slot1")
+        wl = weigh(last, V, acc_t[:, lastj:], "slot3")
+        nc.vector.scalar_tensor_tensor(zz[:], zb[:], 0.5, zy[:], ALU.mult, ALU.add)
+        total(last, V, wl)
+        second_layer(2, y2[:], "slot3")
+        nc.vector.tensor_tensor(terms[:, :, D], zz[:, last:], dsum[:, last:], ALU.subtract)
+        a01 = correct(0, 2 * VC, y01[:])
+        second_layer(3, y3[:], "hc3")
+        w01 = weigh(0, 2 * VC, a01[:], "hg3")
+        a2 = correct(2 * VC, last, y2[:])
+        total(0, 2 * VC, w01)
+        wa2 = weigh(2 * VC, last, a2[:], "wa2")
+        nc.vector.tensor_tensor(terms[:, :, :D], y3[:].rearrange("p (v d) -> p v d", d=D), ycoef[:], ALU.mult)
+        total(2 * VC, last, wa2)
+        nc.vector.tensor_reduce(res[:, last:], terms[:, :, : D + 1], AXIS.X, ALU.add)
         nc.vector.tensor_tensor(res[:, :last], zz[:, :last], dsum[:, :last], ALU.subtract)
-        nc.vector.tensor_tensor(res[:, last:], zz[:, last:], dsum[:, last:], ALU.subtract)
         nc.sync.dma_start(out, res[:])

@@ -14,14 +14,24 @@ AXIS = mybir.AxisListType
 
 P = 128
 PACK = 4
-T, S, H, V, U, D = 1024, 512, 512, 128, 512, 4
+K = P * PACK
+STORE = 1024
+S = 512
+H = 512
+V = 128
+POSES = 512
+D = 4
 CHUNK = 128
 NCHUNK = S // CHUNK
 VC = CHUNK // D
-HALF = H // 2
-MH = HALF // PACK
+QUARTERS = 4
+QCOLS = H // QUARTERS
+QGROUPS = QCOLS // PACK
+VECTOR_GROUPS = QGROUPS // 2
+QUADRANT = 32
+SCALE_ROWS = 4
 
-FLOPS = 2 * 512 * H * S + 2 * H * P * S
+FLOPS = 2 * K * H * S + 2 * H * P * S
 
 
 def tile_picked_yimu_res_p_kernel(
@@ -29,180 +39,182 @@ def tile_picked_yimu_res_p_kernel(
 ):
     nc = tc.nc
     with tc.tile_pool(name="sb", bufs=1) as sb, tc.psum_pool(name="ps", bufs=1) as ps:
+
         offs_t = sb.tile([P, S // 16], U16, name="offs_t")
         from_t = sb.tile([P, V // 16], U16, name="from_t")
         to_t = sb.tile([P, V // 16], U16, name="to_t")
-        xw = sb.tile([P, T], U32, name="xw", align_bytes=64)
-        xs = sb.tile([P, T], U8, name="xs", align_bytes=64)
+        x_win = sb.tile([P, STORE], U32, name="x_win", align_bytes=64)
+        xs_win = sb.tile([P, STORE], U8, name="xs_win", align_bytes=64)
 
-        nc.vector.memset(xs[:].bitcast(I32), 0)
-        xs_in = sb.tile([P, T], U8, name="xs_in", align_bytes=64)
-        for q in range(4):
-            rows = slice(32 * q, 32 * q + 4)
-            queue = nc.sync if q < 2 else nc.scalar
-            queue.dma_start(xs_in[rows, :].bitcast(I32), x_scales[0, 4 * q : 4 * q + 4, :].bitcast(I32))
-            nc.vector.tensor_copy(xs[rows, :].bitcast(I32), xs_in[rows, :].bitcast(I32))
+        nc.vector.memset(xs_win[:].bitcast(I32), 0)
+        lev_v = sb.tile([P, D], F32, name="lev_v")
+        dt_v = sb.tile([P, D], F32, name="dt_v")
+        nc.scalar.dma_start(lev_v[:], lev[0:1, :].rearrange("o (v d) -> (o v) d", d=D))
+        nc.scalar.dma_start(dt_v[:], dt[0:1, :].rearrange("o (v d) -> (o v) d", d=D))
         nc.sync.dma_start(offs_t[:], offs)
-        nc.sync.dma_start(xw[:].bitcast(I32), x_words[0].rearrange("p n t -> p (n t)").bitcast(I32))
-        w1v = w1.rearrange("(p j) c -> p j c", j=PACK)
-        w1a = sb.tile([P, PACK, HALF], F32, name="w1a")
-        w1b = sb.tile([P, PACK, HALF], F32, name="w1b", tag="slot5", align_bytes=64)
-        lev_s = sb.tile([P, D], F32, name="lev_s")
-        dt_s = sb.tile([P, D], F32, name="dt_s")
-        w2raw = sb.tile([P, PACK, P], F32, name="w2raw", tag="slot6", align_bytes=64)
-        tt_t = sb.tile([P, V], F32, name="tt_t")
-        vel_t = sb.tile([P, U], F32, name="vel_t")
-        posi_t = sb.tile([P, U], F32, name="posi_t")
-        acc_t = sb.tile([P, S], F32, name="acc_t")
-        nc.sync.dma_start(w1a[:], w1v[:, :, :HALF])
-        nc.sync.dma_start(lev_s[:], lev[0:1, :].rearrange("o (v d) -> (o v) d", d=D))
-        nc.sync.dma_start(dt_s[:], dt[0:1, :].rearrange("o (v d) -> (o v) d", d=D))
-        nc.sync.dma_start(w1b[:], w1v[:, :, HALF:])
-        nc.sync.dma_start(w2raw[:], w2.rearrange("(p j) m -> p j m", j=PACK))
         nc.sync.dma_start(from_t[:], from1)
-        nc.sync.dma_start(to_t[:], to1)
+        nc.sync.dma_start(x_win[:].bitcast(I32), x_words[0].rearrange("p n t -> p (n t)").bitcast(I32))
+        w1_rows = w1.rearrange("(p j) c -> p j c", j=PACK)
+        w1_raw = []
+        for quarter in range(QUARTERS):
+            raw = sb.tile([P, PACK, QCOLS], F32, name="w1_raw%d" % quarter)
+            nc.sync.dma_start(raw[:], w1_rows[:, :, quarter * QCOLS : (quarter + 1) * QCOLS])
+            w1_raw.append(raw)
+            if quarter == 0:
+                for q in range(P // QUADRANT):
+                    nc.sync.dma_start(
+                        xs_win[QUADRANT * q : QUADRANT * q + SCALE_ROWS, :].bitcast(I32),
+                        x_scales[0, SCALE_ROWS * q : SCALE_ROWS * (q + 1), :].bitcast(I32),
+                    )
+        w2_raw = sb.tile([P, PACK, P], F32, name="w2_raw", tag="reuse_w2_raw", align_bytes=64)
+        tt_t = sb.tile([P, V], F32, name="tt_t")
+        vel_t = sb.tile([P, POSES], F32, name="vel_t")
+        posi_t = sb.tile([P, POSES], F32, name="posi_t")
+        accel_t = sb.tile([P, S], F32, name="accel_t")
+        nc.sync.dma_start(w2_raw[:], w2.rearrange("(p j) m -> p j m", j=PACK))
         nc.sync.dma_start(posi_t[:], posi)
+        nc.sync.dma_start(to_t[:], to1)
         nc.sync.dma_start(tt_t[:], tt)
         nc.sync.dma_start(vel_t[:], vel)
-        nc.sync.dma_start(acc_t[:], accel)
+        nc.sync.dma_start(accel_t[:], accel)
 
         ident = sb.tile([P, P], F32, name="ident")
         make_identity(nc, ident[:])
 
-        gs = sb.tile([P, S], U8, name="gs", align_bytes=64)
-        gw = sb.tile([P, S], U32, name="gw", align_bytes=64)
-        nc.vector.tensor_copy(gs[:], xs[:].indirect(offs_t[:]))
-        nc.vector.tensor_copy(gw[:], xw[:].indirect(offs_t[:]))
+        x_scale = sb.tile([P, S], U8, name="x_scale", align_bytes=64)
+        x_code = sb.tile([P, S], U32, name="x_code", align_bytes=64)
+        nc.vector.tensor_copy(x_code[:], x_win[:].indirect(offs_t[:]))
+        nc.vector.tensor_copy(x_scale[:], xs_win[:].indirect(offs_t[:]))
 
-        w1c = [sb.tile([P, P], U32, name="w1c%d" % t, align_bytes=64) for t in range(PACK)]
-        w1s = [sb.tile([P, P], U8, name="w1s%d" % t, align_bytes=64) for t in range(PACK)]
-        ga = sb.tile([P, PACK - 1, MH, PACK], BF16, name="ga", align_bytes=64)
-        gd = sb.tile([P, MH, PACK], BF16, name="gd", align_bytes=64)
-        gb = sb.tile([P, PACK - 1, MH, PACK], BF16, name="gb", tag="slot0", align_bytes=64)
-        gc = sb.tile([P, MH, PACK], BF16, name="gc", tag="slot1", align_bytes=64)
-        src_a = w1a[:].rearrange("p j (m t) -> p m t j", t=PACK)
-        src_b = w1b[:].rearrange("p j (m t) -> p m t j", t=PACK)
-        nc.scalar.activation(ga[:].rearrange("p t m j -> p m t j"), src_a[:, :, : PACK - 1, :], ACT.Copy)
-        nc.vector.tensor_copy(gd[:], src_a[:, :, PACK - 1, :])
-        nc.vector.tensor_copy(gb[:].rearrange("p t m j -> p m t j"), src_b[:, :, : PACK - 1, :])
-        nc.scalar.activation(gc[:], src_b[:, :, PACK - 1, :], ACT.Copy)
-        for half in range(2):
-            for t in range(PACK):
-                cols = slice(half * MH, (half + 1) * MH)
-                grouped = (ga, gb)[half][:, t] if t < PACK - 1 else (gd, gc)[half][:]
-                nc.vector.quantize_mx(
-                    out=w1c[t][:, cols].bitcast(FP8X4),
-                    scales=w1s[t][:, cols],
-                    in_=grouped.rearrange("p m j -> p (m j)"),
-                )
+        w1_code = [sb.tile([P, P], U32, name="w1_code%d" % t, align_bytes=64) for t in range(PACK)]
+        w1_scale = [sb.tile([P, P], U8, name="w1_scale%d" % t, align_bytes=64) for t in range(PACK)]
+        w1_bf = sb.tile([P, PACK, P, PACK], BF16, name="w1_bf", tag="reuse_w1_bf", align_bytes=64)
+        dealt = w1_bf[:].rearrange("p t m j -> p m t j")
+        for quarter in range(QUARTERS):
+            groups = w1_raw[quarter][:].rearrange("p j (m t) -> p m t j", t=PACK)
+            m0 = quarter * QGROUPS
+            split = VECTOR_GROUPS if quarter == QUARTERS - 1 else 0
+            if split:
+                nc.vector.tensor_copy(dealt[:, m0 : m0 + split], groups[:, :split])
+            nc.scalar.activation(dealt[:, m0 + split : m0 + QGROUPS], groups[:, split:], ACT.Copy)
+        for t in range(PACK):
+            nc.vector.quantize_mx(
+                out=w1_code[t][:].bitcast(FP8X4),
+                scales=w1_scale[t][:],
+                in_=w1_bf[:, t, :, :].rearrange("p m j -> p (m j)"),
+            )
 
-        w2g = sb.tile([P, P, PACK], BF16, name="w2g", tag="slot5", align_bytes=64)
+        w2_bf = sb.tile([P, P, PACK], BF16, name="w2_bf", align_bytes=64)
         nc.scalar.activation(
-            w2g[:].rearrange("p (c i) j -> p c j i", i=4),
-            w2raw[:].rearrange("p j (c i) -> p c j i", i=4),
+            w2_bf[:].rearrange("p (c i) j -> p c j i", i=PACK),
+            w2_raw[:].rearrange("p j (c i) -> p c j i", i=PACK),
             ACT.Copy,
         )
-        w2c = sb.tile([P, P], U32, name="w2c", align_bytes=64)
-        w2s = sb.tile([P, P], U8, name="w2s", align_bytes=64)
-        nc.vector.quantize_mx(out=w2c[:].bitcast(FP8X4), scales=w2s[:], in_=w2g[:].rearrange("p m j -> p (m j)"))
+        w2_code = sb.tile([P, P], U32, name="w2_code", align_bytes=64)
+        w2_scale = sb.tile([P, P], U8, name="w2_scale", align_bytes=64)
+        nc.vector.quantize_mx(
+            out=w2_code[:].bitcast(FP8X4), scales=w2_scale[:], in_=w2_bf[:].rearrange("p m j -> p (m j)")
+        )
 
-        coef_s = sb.tile([P, D], F32, name="coef_s")
+        weight_v = sb.tile([P, D], F32, name="weight_v")
         half_dt = sb.tile([P, D], F32, name="half_dt")
-        nc.gpsimd.tensor_scalar(half_dt[:], dt_s[:], 0.5, 0.0, ALU.mult, ALU.add)
-        nc.gpsimd.tensor_tensor(coef_s[:], half_dt[:], lev_s[:], ALU.add)
-        coef = ps.tile([P, D, V], F32, name="coef")
+        nc.gpsimd.tensor_scalar(half_dt[:], dt_v[:], 0.5, 0.0, ALU.mult, ALU.add)
+        nc.gpsimd.tensor_tensor(weight_v[:], half_dt[:], lev_v[:], ALU.add)
+        weight = ps.tile([P, D, V], F32, name="weight")
         for d in range(D):
-            nc.tensor.transpose(coef[:, d, :], coef_s[:, d : d + 1].to_broadcast([P, P]), ident[:])
-        tt2 = sb.tile([P, V], F32, name="tt2")
-        nc.gpsimd.tensor_scalar(tt2[:], tt_t[:], 2.0, 1.0, ALU.mult, ALU.add)
-        last = (NCHUNK - 1) * VC
-        lastj = (NCHUNK - 1) * CHUNK
-        coef_last = coef[:, :, last:].rearrange("p d v -> p v d")
-        ycoef = sb.tile([P, VC, D], F32, name="ycoef", tag="slot6", align_bytes=64)
-        nc.scalar.activation(ycoef[:], coef_last, ACT.Copy, scale=-0.3)
+            nc.tensor.transpose(weight[:, d, :], weight_v[:, d : d + 1].to_broadcast([P, P]), ident[:])
+        tt_factor = sb.tile([P, V], F32, name="tt_factor")
+        nc.gpsimd.tensor_scalar(tt_factor[:], tt_t[:], 2.0, 1.0, ALU.mult, ALU.add)
+        v_last = (NCHUNK - 1) * VC
+        y_factor = sb.tile([P, VC, D], F32, name="y_factor", tag="reuse_w2_raw", align_bytes=64)
+        nc.scalar.activation(y_factor[:], weight[:, :, v_last:].rearrange("p d v -> p v d"), ACT.Copy, scale=-0.3)
 
-        hg = []
+        h_bf01 = sb.tile([P, 2 * CHUNK, PACK], BF16, name="h_bf01", align_bytes=64)
+        h_bf2 = sb.tile([P, CHUNK, PACK], BF16, name="h_bf2", align_bytes=64)
+        h_bf3 = sb.tile([P, CHUNK, PACK], BF16, name="h_bf3", tag="reuse_h_bf3", align_bytes=64)
+        h_bf = [h_bf01[:, :CHUNK, :], h_bf01[:, CHUNK:, :], h_bf2[:], h_bf3[:]]
         for c in range(NCHUNK):
             cols = slice(c * CHUNK, (c + 1) * CHUNK)
-            hp = ps.tile([P, PACK, CHUNK], F32, name="hp%d" % c, tag="bank%d" % c)
+            h_ps = ps.tile([P, PACK, CHUNK], F32, name="h_ps%d" % c, tag="bank%d" % c)
             for t in range(PACK):
                 nc.tensor.matmul_mx(
-                    out=hp[:, t, :],
-                    lhsT=w1c[t][:].bitcast(FP8X4),
-                    lhsT_scale=w1s[t][:],
-                    rhs=gw[:, cols].bitcast(FP8X4),
-                    rhs_scale=gs[:, cols],
+                    out=h_ps[:, t, :],
+                    lhsT=w1_code[t][:].bitcast(FP8X4),
+                    lhsT_scale=w1_scale[t][:],
+                    rhs=x_code[:, cols].bitcast(FP8X4),
+                    rhs_scale=x_scale[:, cols],
                     start=True,
                     stop=True,
                 )
-            g = sb.tile([P, CHUNK, PACK], BF16, name="hg%d" % c, tag="hg%d" % c, align_bytes=64)
-            nc.scalar.activation(g[:], hp[:].rearrange("p t n -> p n t"), ACT.Relu)
-            hg.append(g)
+            nc.scalar.activation(h_bf[c], h_ps[:].rearrange("p t n -> p n t"), ACT.Relu)
 
-        za = sb.tile([P, V], F32, name="za", tag="slot1", align_bytes=64)
-        zx = sb.tile([P, V], F32, name="zx", tag="slot0", align_bytes=64)
-        zb = sb.tile([P, V], F32, name="zb")
-        zy = sb.tile([P, V], F32, name="zy")
-        zz = sb.tile([P, V], F32, name="zz")
-        nc.vector.tensor_copy(zx[:], posi_t[:].indirect(from_t[:]))
-        nc.vector.tensor_tensor(zy[:], posi_t[:].indirect(to_t[:]), zx[:], ALU.subtract)
+        vel_from = sb.tile([P, V], F32, name="vel_from", tag="reuse_vel_from", align_bytes=64)
+        posi_from = sb.tile([P, V], F32, name="posi_from", tag="reuse_w1_bf", align_bytes=64)
+        vel_diff = sb.tile([P, V], F32, name="vel_diff")
+        posi_diff = sb.tile([P, V], F32, name="posi_diff")
+        pose = sb.tile([P, V], F32, name="pose")
+        nc.vector.tensor_copy(posi_from[:], posi_t[:].indirect(from_t[:]))
+        nc.vector.tensor_tensor(posi_diff[:], posi_t[:].indirect(to_t[:]), posi_from[:], ALU.subtract)
 
-        def second_layer(c, yp, codes_tag):
-            hc = sb.tile([P, CHUNK], U32, name="hc%d" % c, tag=codes_tag, align_bytes=64)
-            hs = sb.tile([P, CHUNK], U8, name="hs%d" % c, align_bytes=64)
-            nc.vector.quantize_mx(out=hc[:].bitcast(FP8X4), scales=hs[:], in_=hg[c][:].rearrange("p n t -> p (n t)"))
+        def second_layer(name, h_part, y_ps, code_tag, scale_tag):
+            width = h_part.shape[1]
+            h_code = sb.tile([P, width], U32, name="h_code" + name, tag=code_tag, align_bytes=64)
+            h_scale = sb.tile([P, width], U8, name="h_scale" + name, tag=scale_tag, align_bytes=64)
+            nc.vector.quantize_mx(
+                out=h_code[:].bitcast(FP8X4), scales=h_scale[:], in_=h_part.rearrange("p n t -> p (n t)")
+            )
             nc.tensor.matmul_mx(
-                out=yp,
-                lhsT=w2c[:].bitcast(FP8X4),
-                lhsT_scale=w2s[:],
-                rhs=hc[:].bitcast(FP8X4),
-                rhs_scale=hs[:],
+                out=y_ps,
+                lhsT=w2_code[:].bitcast(FP8X4),
+                lhsT_scale=w2_scale[:],
+                rhs=h_code[:].bitcast(FP8X4),
+                rhs_scale=h_scale[:],
                 start=True,
                 stop=True,
             )
 
-        dsum = sb.tile([P, V], F32, name="dsum")
+        sums = sb.tile([P, V], F32, name="sums")
         res = sb.tile([P, V], F32, name="res")
         terms = sb.tile([P, VC, 2 * D], F32, name="terms")
 
-        def correct(v0, v1, yp):
-            a0 = sb.tile([P, (v1 - v0) * D], F32, name="a0_%d" % v0, tag="a0")
-            nc.vector.scalar_tensor_tensor(a0[:], yp, 0.3, acc_t[:, v0 * D : v1 * D], ALU.mult, ALU.add)
-            return a0
+        def correct(v0, v1, y_ps):
+            corrected = sb.tile([P, (v1 - v0) * D], F32, name="corrected%d" % v0, tag="reuse_corrected")
+            nc.vector.scalar_tensor_tensor(corrected[:], y_ps, 0.3, accel_t[:, v0 * D : v1 * D], ALU.mult, ALU.add)
+            return corrected
 
         def weigh(v0, v1, values, tag):
-            wa = sb.tile([P, v1 - v0, D], F32, name="wa%d" % v0, tag=tag, align_bytes=64)
+            weighed = sb.tile([P, v1 - v0, D], F32, name="weighed%d" % v0, tag=tag, align_bytes=64)
             nc.vector.tensor_tensor(
-                wa[:],
+                weighed[:],
                 values.rearrange("p (v d) -> p v d", d=D),
-                coef[:, :, v0:v1].rearrange("p d v -> p v d"),
+                weight[:, :, v0:v1].rearrange("p d v -> p v d"),
                 ALU.mult,
             )
-            return wa
+            return weighed
 
-        def total(v0, v1, wa):
-            nc.vector.tensor_reduce(dsum[:, v0:v1], wa[:], AXIS.X, ALU.add)
+        def add_up(v0, v1, weighed):
+            nc.vector.tensor_reduce(sums[:, v0:v1], weighed[:], AXIS.X, ALU.add)
 
+        v_mid = 2 * VC
         y01 = ps.tile([P, 2 * CHUNK], F32, name="y01", tag="bank0")
         y2 = ps.tile([P, CHUNK], F32, name="y2", tag="bank1")
         y3 = ps.tile([P, CHUNK], F32, name="y3", tag="bank2")
-        nc.vector.tensor_tensor(za[:], vel_t[:].indirect(from_t[:]), tt2[:], ALU.mult)
-        second_layer(0, y01[:, :CHUNK], "slot0")
-        nc.vector.tensor_tensor(zb[:], vel_t[:].indirect(to_t[:]), za[:], ALU.subtract)
-        second_layer(1, y01[:, CHUNK:], "slot1")
-        wl = weigh(last, V, acc_t[:, lastj:], "slot3")
-        nc.vector.scalar_tensor_tensor(zz[:], zb[:], 0.5, zy[:], ALU.mult, ALU.add)
-        total(last, V, wl)
-        second_layer(2, y2[:], "slot3")
-        nc.vector.tensor_tensor(terms[:, :, D], zz[:, last:], dsum[:, last:], ALU.subtract)
-        a01 = correct(0, 2 * VC, y01[:])
-        second_layer(3, y3[:], "hc3")
-        w01 = weigh(0, 2 * VC, a01[:], "hg3")
-        a2 = correct(2 * VC, last, y2[:])
-        total(0, 2 * VC, w01)
-        wa2 = weigh(2 * VC, last, a2[:], "wa2")
-        nc.vector.tensor_tensor(terms[:, :, :D], y3[:].rearrange("p (v d) -> p v d", d=D), ycoef[:], ALU.mult)
-        total(2 * VC, last, wa2)
-        nc.vector.tensor_reduce(res[:, last:], terms[:, :, : D + 1], AXIS.X, ALU.add)
-        nc.vector.tensor_tensor(res[:, :last], zz[:, :last], dsum[:, :last], ALU.subtract)
+        nc.vector.tensor_tensor(vel_from[:], vel_t[:].indirect(from_t[:]), tt_factor[:], ALU.mult)
+        nc.vector.tensor_tensor(vel_diff[:], vel_t[:].indirect(to_t[:]), vel_from[:], ALU.subtract)
+        second_layer("01", h_bf01[:], y01[:], "reuse_w1_bf", "reuse_vel_from")
+        accel_last = weigh(v_last, V, accel_t[:, v_last * D :], "reuse_accel_last")
+        nc.vector.scalar_tensor_tensor(pose[:], vel_diff[:], 0.5, posi_diff[:], ALU.mult, ALU.add)
+        add_up(v_last, V, accel_last)
+        second_layer("2", h_bf2[:], y2[:], "reuse_accel_last", "h_scale2")
+        nc.vector.tensor_tensor(terms[:, :, D], pose[:, v_last:], sums[:, v_last:], ALU.subtract)
+        corrected01 = correct(0, v_mid, y01[:])
+        second_layer("3", h_bf3[:], y3[:], "h_code3", "h_scale3")
+        weighed01 = weigh(0, v_mid, corrected01[:], "reuse_h_bf3")
+        corrected2 = correct(v_mid, v_last, y2[:])
+        add_up(0, v_mid, weighed01)
+        weighed2 = weigh(v_mid, v_last, corrected2[:], "weighed2")
+        nc.vector.tensor_tensor(terms[:, :, :D], y3[:].rearrange("p (v d) -> p v d", d=D), y_factor[:], ALU.mult)
+        add_up(v_mid, v_last, weighed2)
+        nc.vector.tensor_reduce(res[:, v_last:], terms[:, :, : D + 1], AXIS.X, ALU.add)
+        nc.vector.tensor_tensor(res[:, :v_last], pose[:, :v_last], sums[:, :v_last], ALU.subtract)
         nc.sync.dma_start(out, res[:])

@@ -177,8 +177,8 @@ def tile_picked_yimu_res_p_kernel(
         res = sb.tile([P, V], F32, name="res")
         terms = sb.tile([P, VC, 2 * D], F32, name="terms")
 
-        def correct(v0, v1, y_ps):
-            corrected = sb.tile([P, (v1 - v0) * D], F32, name="corrected%d" % v0, tag="reuse_corrected")
+        def correct(v0, v1, y_ps, tag):
+            corrected = sb.tile([P, (v1 - v0) * D], F32, name="corrected%d" % v0, tag=tag, align_bytes=64)
             nc.vector.scalar_tensor_tensor(corrected[:], y_ps, 0.3, accel_t[:, v0 * D : v1 * D], ALU.mult, ALU.add)
             return corrected
 
@@ -207,12 +207,12 @@ def tile_picked_yimu_res_p_kernel(
         add_up(v_last, V, accel_last)
         second_layer("2", h_bf2[:], y2[:], "reuse_accel_last", "h_scale2")
         nc.vector.tensor_tensor(terms[:, :, D], pose[:, v_last:], sums[:, v_last:], ALU.subtract)
-        corrected01 = correct(0, v_mid, y01[:])
         second_layer("3", h_bf3[:], y3[:], "h_code3", "h_scale3")
-        weighed01 = weigh(0, v_mid, corrected01[:], "reuse_h_bf3")
-        corrected2 = correct(v_mid, v_last, y2[:])
-        add_up(0, v_mid, weighed01)
+        corrected01 = correct(0, v_mid, y01[:], "reuse_h_bf3")
+        corrected2 = correct(v_mid, v_last, y2[:], "corrected2")
+        weighed01 = weigh(0, v_mid, corrected01[:], "weighed01")
         weighed2 = weigh(v_mid, v_last, corrected2[:], "weighed2")
+        add_up(0, v_mid, weighed01)
         nc.vector.tensor_tensor(terms[:, :, :D], y3[:].rearrange("p (v d) -> p v d", d=D), y_factor[:], ALU.mult)
         add_up(v_mid, v_last, weighed2)
         nc.vector.tensor_reduce(res[:, v_last:], terms[:, :, : D + 1], AXIS.X, ALU.add)

import concourse.mybir as mybir
from concourse.masks import make_identity

F32 = mybir.dt.float32
BF16 = mybir.dt.bfloat16
I32 = mybir.dt.int32
U32 = mybir.dt.uint32
U16 = mybir.dt.uint16
U8 = mybir.dt.uint8
FP8X4 = mybir.dt.float8_e4m3fn_x4
ALU = mybir.AluOpType
ACT = mybir.ActivationFunctionType
AXIS = mybir.AxisListType

P = 128
PACK = 4
K = P * PACK
STORE = 1024
S = 512
H = 512
V = 128
POSES = 512
D = 4
CHUNK = 128
NCHUNK = S // CHUNK
VC = CHUNK // D
QUARTERS = 4
QCOLS = H // QUARTERS
QGROUPS = QCOLS // PACK
VECTOR_GROUPS = QGROUPS // 2
QUADRANT = 32
SCALE_ROWS = 4

FLOPS = 2 * K * H * S + 2 * H * P * S


def tile_picked_yimu_res_p_kernel(
    tc, x_words, x_scales, w1, w2, accel, dt, lev, vel, posi, tt, offs, from1, to1, out
):
    nc = tc.nc
    with tc.tile_pool(name="sb", bufs=1) as sb, tc.psum_pool(name="ps", bufs=1) as ps:

        offs_t = sb.tile([P, S // 16], U16, name="offs_t")
        from_t = sb.tile([P, V // 16], U16, name="from_t")
        to_t = sb.tile([P, V // 16], U16, name="to_t")
        x_win = sb.tile([P, STORE], U32, name="x_win", align_bytes=64)
        xs_win = sb.tile([P, STORE], U8, name="xs_win", align_bytes=64)

        nc.vector.memset(xs_win[:].bitcast(I32), 0)
        lev_v = sb.tile([P, D], F32, name="lev_v")
        dt_v = sb.tile([P, D], F32, name="dt_v")
        nc.scalar.dma_start(lev_v[:], lev[0:1, :].rearrange("o (v d) -> (o v) d", d=D))
        nc.scalar.dma_start(dt_v[:], dt[0:1, :].rearrange("o (v d) -> (o v) d", d=D))
        nc.sync.dma_start(offs_t[:], offs)
        nc.sync.dma_start(from_t[:], from1)
        nc.sync.dma_start(x_win[:].bitcast(I32), x_words[0].rearrange("p n t -> p (n t)").bitcast(I32))
        w1_rows = w1.rearrange("(p j) c -> p j c", j=PACK)
        w1_raw = []
        for quarter in range(QUARTERS):
            raw = sb.tile([P, PACK, QCOLS], F32, name="w1_raw%d" % quarter)
            nc.sync.dma_start(raw[:], w1_rows[:, :, quarter * QCOLS : (quarter + 1) * QCOLS])
            w1_raw.append(raw)
            if quarter == 0:
                for q in range(P // QUADRANT):
                    nc.sync.dma_start(
                        xs_win[QUADRANT * q : QUADRANT * q + SCALE_ROWS, :].bitcast(I32),
                        x_scales[0, SCALE_ROWS * q : SCALE_ROWS * (q + 1), :].bitcast(I32),
                    )
        w2_raw = sb.tile([P, PACK, P], F32, name="w2_raw", tag="reuse_w2_raw", align_bytes=64)
        tt_t = sb.tile([P, V], F32, name="tt_t")
        vel_t = sb.tile([P, POSES], F32, name="vel_t")
        posi_t = sb.tile([P, POSES], F32, name="posi_t")
        accel_t = sb.tile([P, S], F32, name="accel_t")
        nc.sync.dma_start(w2_raw[:], w2.rearrange("(p j) m -> p j m", j=PACK))
        nc.sync.dma_start(posi_t[:], posi)
        nc.sync.dma_start(to_t[:], to1)
        nc.sync.dma_start(tt_t[:], tt)
        nc.sync.dma_start(vel_t[:], vel)
        nc.sync.dma_start(accel_t[:], accel)

        ident = sb.tile([P, P], F32, name="ident")
        make_identity(nc, ident[:])

        x_scale = sb.tile([P, S], U8, name="x_scale", align_bytes=64)
        x_code = sb.tile([P, S], U32, name="x_code", align_bytes=64)
        nc.vector.tensor_copy(x_code[:], x_win[:].indirect(offs_t[:]))
        nc.vector.tensor_copy(x_scale[:], xs_win[:].indirect(offs_t[:]))

        w1_code = [sb.tile([P, P], U32, name="w1_code%d" % t, align_bytes=64) for t in range(PACK)]
        w1_scale = [sb.tile([P, P], U8, name="w1_scale%d" % t, align_bytes=64) for t in range(PACK)]
        w1_bf = sb.tile([P, PACK, P, PACK], BF16, name="w1_bf", tag="reuse_w1_bf", align_bytes=64)
        dealt = w1_bf[:].rearrange("p t m j -> p m t j")
        for quarter in range(QUARTERS):
            groups = w1_raw[quarter][:].rearrange("p j (m t) -> p m t j", t=PACK)
            m0 = quarter * QGROUPS
            split = VECTOR_GROUPS if quarter == QUARTERS - 1 else 0
            if split:
                nc.vector.tensor_copy(dealt[:, m0 : m0 + split], groups[:, :split])
            nc.scalar.activation(dealt[:, m0 + split : m0 + QGROUPS], groups[:, split:], ACT.Copy)
        for t in range(PACK):
            nc.vector.quantize_mx(
                out=w1_code[t][:].bitcast(FP8X4),
                scales=w1_scale[t][:],
                in_=w1_bf[:, t, :, :].rearrange("p m j -> p (m j)"),
            )

        w2_bf = sb.tile([P, P, PACK], BF16, name="w2_bf", align_bytes=64)
        nc.scalar.activation(
            w2_bf[:].rearrange("p (c i) j -> p c j i", i=PACK),
            w2_raw[:].rearrange("p j (c i) -> p c j i", i=PACK),
            ACT.Copy,
        )
        w2_code = sb.tile([P, P], U32, name="w2_code", align_bytes=64)
        w2_scale = sb.tile([P, P], U8, name="w2_scale", align_bytes=64)
        nc.vector.quantize_mx(
            out=w2_code[:].bitcast(FP8X4), scales=w2_scale[:], in_=w2_bf[:].rearrange("p m j -> p (m j)")
        )

        weight_v = sb.tile([P, D], F32, name="weight_v")
        half_dt = sb.tile([P, D], F32, name="half_dt")
        nc.gpsimd.tensor_scalar(half_dt[:], dt_v[:], 0.5, 0.0, ALU.mult, ALU.add)
        nc.gpsimd.tensor_tensor(weight_v[:], half_dt[:], lev_v[:], ALU.add)
        weight = ps.tile([P, D, V], F32, name="weight")
        for d in range(D):
            nc.tensor.transpose(weight[:, d, :], weight_v[:, d : d + 1].to_broadcast([P, P]), ident[:])
        tt_factor = sb.tile([P, V], F32, name="tt_factor")
        nc.gpsimd.tensor_scalar(tt_factor[:], tt_t[:], 2.0, 1.0, ALU.mult, ALU.add)
        v_last = (NCHUNK - 1) * VC
        y_factor = sb.tile([P, VC, D], F32, name="y_factor", tag="reuse_w2_raw", align_bytes=64)
        nc.scalar.activation(y_factor[:], weight[:, :, v_last:].rearrange("p d v -> p v d"), ACT.Copy, scale=-0.3)

        h_bf01 = sb.tile([P, 2 * CHUNK, PACK], BF16, name="h_bf01", align_bytes=64)
        h_bf2 = sb.tile([P, CHUNK, PACK], BF16, name="h_bf2", align_bytes=64)
        h_bf3 = sb.tile([P, CHUNK, PACK], BF16, name="h_bf3", tag="reuse_h_bf3", align_bytes=64)
        h_bf = [h_bf01[:, :CHUNK, :], h_bf01[:, CHUNK:, :], h_bf2[:], h_bf3[:]]
        for c in range(NCHUNK):
            cols = slice(c * CHUNK, (c + 1) * CHUNK)
            h_ps = ps.tile([P, PACK, CHUNK], F32, name="h_ps%d" % c, tag="bank%d" % c)
            for t in range(PACK):
                nc.tensor.matmul_mx(
                    out=h_ps[:, t, :],
                    lhsT=w1_code[t][:].bitcast(FP8X4),
                    lhsT_scale=w1_scale[t][:],
                    rhs=x_code[:, cols].bitcast(FP8X4),
                    rhs_scale=x_scale[:, cols],
                    start=True,
                    stop=True,
                )
            nc.scalar.activation(h_bf[c], h_ps[:].rearrange("p t n -> p n t"), ACT.Relu)

        vel_from = sb.tile([P, V], F32, name="vel_from", tag="reuse_vel_from", align_bytes=64)
        posi_from = sb.tile([P, V], F32, name="posi_from", tag="reuse_w1_bf", align_bytes=64)
        vel_diff = sb.tile([P, V], F32, name="vel_diff")
        posi_diff = sb.tile([P, V], F32, name="posi_diff")
        pose = sb.tile([P, V], F32, name="pose")
        nc.vector.tensor_copy(posi_from[:], posi_t[:].indirect(from_t[:]))
        nc.vector.tensor_tensor(posi_diff[:], posi_t[:].indirect(to_t[:]), posi_from[:], ALU.subtract)

        def second_layer(name, h_part, y_ps, code_tag, scale_tag):
            width = h_part.shape[1]
            h_code = sb.tile([P, width], U32, name="h_code" + name, tag=code_tag, align_bytes=64)
            h_scale = sb.tile([P, width], U8, name="h_scale" + name, tag=scale_tag, align_bytes=64)
            nc.vector.quantize_mx(
                out=h_code[:].bitcast(FP8X4), scales=h_scale[:], in_=h_part.rearrange("p n t -> p (n t)")
            )
            nc.tensor.matmul_mx(
                out=y_ps,
                lhsT=w2_code[:].bitcast(FP8X4),
                lhsT_scale=w2_scale[:],
                rhs=h_code[:].bitcast(FP8X4),
                rhs_scale=h_scale[:],
                start=True,
                stop=True,
            )

        sums = sb.tile([P, V], F32, name="sums")
        res = sb.tile([P, V], F32, name="res")
        terms = sb.tile([P, VC, 2 * D], F32, name="terms")

        def correct(v0, v1, y_ps, tag):
            corrected = sb.tile([P, (v1 - v0) * D], F32, name="corrected%d" % v0, tag=tag, align_bytes=64)
            nc.vector.scalar_tensor_tensor(corrected[:], y_ps, 0.3, accel_t[:, v0 * D : v1 * D], ALU.mult, ALU.add)
            return corrected

        def weigh(v0, v1, values, tag):
            weighed = sb.tile([P, v1 - v0, D], F32, name="weighed%d" % v0, tag=tag, align_bytes=64)
            nc.vector.tensor_tensor(
                weighed[:],
                values.rearrange("p (v d) -> p v d", d=D),
                weight[:, :, v0:v1].rearrange("p d v -> p v d"),
                ALU.mult,
            )
            return weighed

        def add_up(v0, v1, weighed):
            nc.vector.tensor_reduce(sums[:, v0:v1], weighed[:], AXIS.X, ALU.add)

        v_mid = 2 * VC
        y01 = ps.tile([P, 2 * CHUNK], F32, name="y01", tag="bank0")
        y2 = ps.tile([P, CHUNK], F32, name="y2", tag="bank1")
        y3 = ps.tile([P, CHUNK], F32, name="y3", tag="bank2")
        nc.vector.tensor_tensor(vel_from[:], vel_t[:].indirect(from_t[:]), tt_factor[:], ALU.mult)
        nc.vector.tensor_tensor(vel_diff[:], vel_t[:].indirect(to_t[:]), vel_from[:], ALU.subtract)
        second_layer("01", h_bf01[:], y01[:], "reuse_w1_bf", "reuse_vel_from")
        accel_last = weigh(v_last, V, accel_t[:, v_last * D :], "reuse_accel_last")
        nc.vector.scalar_tensor_tensor(pose[:], vel_diff[:], 0.5, posi_diff[:], ALU.mult, ALU.add)
        add_up(v_last, V, accel_last)
        second_layer("2", h_bf2[:], y2[:], "reuse_accel_last", "h_scale2")
        nc.vector.tensor_tensor(terms[:, :, D], pose[:, v_last:], sums[:, v_last:], ALU.subtract)
        second_layer("3", h_bf3[:], y3[:], "h_code3", "h_scale3")
        corrected01 = correct(0, v_mid, y01[:], "reuse_h_bf3")
        corrected2 = correct(v_mid, v_last, y2[:], "corrected2")
        weighed01 = weigh(0, v_mid, corrected01[:], "weighed01")
        weighed2 = weigh(v_mid, v_last, corrected2[:], "weighed2")
        add_up(0, v_mid, weighed01)
        nc.vector.tensor_tensor(terms[:, :, :D], y3[:].rearrange("p (v d) -> p v d", d=D), y_factor[:], ALU.mult)
        add_up(v_mid, v_last, weighed2)
        nc.vector.tensor_reduce(res[:, v_last:], terms[:, :, : D + 1], AXIS.X, ALU.add)
        nc.vector.tensor_tensor(res[:, :v_last], pose[:, :v_last], sums[:, :v_last], ALU.subtract)
        nc.sync.dma_start(out, res[:])
